import numpy as np
import ml_dtypes


def mxq(x, axis, fmt="e4m3"):
    dtype, down = {"e4m3": (ml_dtypes.float8_e4m3fn, 7), "e5m2": (ml_dtypes.float8_e5m2, 14)}[fmt]
    v = np.moveaxis(np.asarray(x, np.float32).astype(ml_dtypes.bfloat16).astype(np.float64), axis, -1)
    blocks = v.reshape(v.shape[:-1] + (-1, 32))
    amax = np.abs(blocks).max(-1, keepdims=True)
    byte = np.maximum(np.where(amax > 0, np.frexp(amax)[1] - 1 + 127, 0) - down, 1)
    scale = np.exp2(byte - 127.0)
    codes = (blocks / scale).astype(np.float32).astype(dtype).astype(np.float64)
    return np.moveaxis((codes * scale).reshape(v.shape), -1, axis)


WIDE = False


def mx_kscale(k):
    if not WIDE:
        return np.ones(k)
    levels = np.array([10, -10, 5, -5, 0])
    if k % 512:
        return np.exp2(np.random.permutation(np.resize(levels, k // 32))).repeat(32)
    a = np.empty((k // 512, 16))
    for p in range(k // 512):
        a[p, :8] = np.random.permutation(np.resize(levels, 8))
        for g in range(8):
            far = levels[np.abs(levels - a[p, g]) >= 10]
            a[p, g + 8] = far[np.random.randint(len(far))]
    return np.exp2(a.ravel()).repeat(32)


def f64(x):
    return np.asarray(x).astype(np.float64)


def striped(idx):
    return np.tile(idx.reshape(-1, 16).T, (8, 1)).astype(np.uint16)


def unstriped(offs):
    return offs[:16].T.reshape(-1).astype(np.int64)


def striped8(idx):
    return np.concatenate([x.reshape(-1, 16).T for x in idx]).astype(np.uint16)


def runs(offs, k):
    lists = np.stack([offs[16 * r : 16 * r + 16].T.reshape(-1) for r in range(8)]).astype(np.int64)
    return lists[np.arange(k) % 512 // 64]


def pack_weight(w):
    k, n = w.shape
    w = f64(np.asarray(w, np.float32).astype(ml_dtypes.bfloat16)).reshape(k // 32, 32, n)
    amax = np.abs(w).max(1)
    byte = np.clip(np.where(amax > 0, np.frexp(amax)[1] - 1 + 127 - 7, 1), 1, 254)
    scaled = (w * np.exp2(127.0 - byte)[:, None, :]).reshape(k, n).astype(np.float32)
    words = np.ascontiguousarray(scaled.reshape(k // 512, 128, 4, n).transpose(0, 1, 3, 2)).astype(ml_dtypes.float8_e4m3fn).view(np.uint8)
    return words, np.ascontiguousarray(byte.astype(np.uint8).reshape(k // 512, 16, n))


def unpack_weight(words, scales):
    g, p, n, _ = words.shape
    vals = np.ascontiguousarray(words).view(ml_dtypes.float8_e4m3fn).astype(np.float64) * np.repeat(np.exp2(scales.astype(np.float64) - 127.0), 8, axis=1)[..., None]
    return vals.transpose(0, 1, 3, 2).reshape(g * 512, n)

def planes(y):
    n, m = y.shape
    v = y.astype(np.float32).astype(ml_dtypes.bfloat16).astype(np.float64).reshape(n // 32, 32, m)
    top = np.abs(v).max(1)
    byte = np.clip(np.where(top > 0, np.frexp(top)[1] - 1 + 127 - 7, 1), 1, 254)
    codes = (v * np.exp2(127.0 - byte)[:, None, :]).reshape(n, m).astype(np.float32).astype(ml_dtypes.float8_e4m3fn).view(np.uint8)
    words = codes.reshape(n // 512, 128, 4, m).transpose(0, 1, 3, 2)
    return np.ascontiguousarray(words), np.ascontiguousarray(byte.astype(np.uint8).reshape(n // 512, 16, m))


K, T, S, N, H = 512, 2048, 512, 512, 512


def setup_inputs():
    n = np.random.standard_normal
    s = mx_kscale(K)[:, None]
    u = mx_kscale(S)
    packed_xT = pack_weight(n((K, T)) * s)
    packed_w1 = pack_weight(n((S, N)) / np.sqrt(S) / u[:, None])
    return {
        "x_words": packed_xT[0],
        "x_scales": packed_xT[1],
        "wa": (n((K, H)) / np.sqrt(K) / s).astype(np.float32),
        "wb": (n((K, H)) / np.sqrt(K) / s).astype(np.float32),
        "gt": (np.random.uniform(0.5, 1.5, (S, 1)) * u[:, None]).astype(np.float32),
        "w1_words": packed_w1[0],
        "w1_scales": packed_w1[1],
        "offs": striped(np.random.permutation(T)[:S]),
        "two": striped(np.random.permutation(T)[:S]),
        "n1": striped(np.random.permutation(H)),
        "n2": striped(np.random.permutation(H)),
        "n3": striped8(np.stack([np.random.permutation(H) for _ in range(8)])),
        "n4": striped8(np.stack([np.random.permutation(H) for _ in range(8)])),
    }


def reference(x_words, x_scales, wa, wb, gt, w1_words, w1_scales, offs, two, n1, n2, n3, n4):
    xq = unpack_weight(x_words, x_scales)[:, unstriped(offs)]
    y = xq.T @ mxq(f64(wa), 0, "e4m3")
    x_two = unpack_weight(x_words, x_scales)[:, unstriped(two)]
    d = x_two.T @ mxq(f64(wb), 0, "e4m3")
    z = f64(gt) * (0.75 * (y * d[:, unstriped(n2)] - (y[:, unstriped(n1)] * d)))
    h = unpack_weight(w1_words, w1_scales).T @ mxq(z, 0, "e4m3")
    out_0 = (h * (h[np.arange(N)[:, None], runs(n3, N)])) * (np.tanh(h[np.arange(N)[:, None], runs(n4, N)]))
    return (out_0,) + planes(out_0)

@@ -1,0 +1,209 @@
+from contextlib import ExitStack
+
+import concourse.mybir as mybir
+
+K, T, S, N, H = 512, 2048, 512, 512, 512
+FLOPS = 2 * K * S * H * 2 + 2 * S * N * H
+
+F32 = mybir.dt.float32
+BF16 = mybir.dt.bfloat16
+I32 = mybir.dt.int32
+U32 = mybir.dt.uint32
+U16 = mybir.dt.uint16
+U8 = mybir.dt.uint8
+FP8X4 = mybir.dt.float8_e4m3fn_x4
+ALU = mybir.AluOpType
+ACT = mybir.ActivationFunctionType
+
+P = 128
+PACK = 4
+HALF = 256
+HALVES = H // HALF
+STRIPE = 16
+
+
+def tile_picked_twtcrossbcube_none_po_kernel(
+    tc, x_words, x_scales, wa, wb, gt, w1_words, w1_scales, offs, two, n1, n2, n3, n4, out_0, out_1, out_2
+):
+    nc = tc.nc
+    with ExitStack() as ctx:
+        keep = ctx.enter_context(tc.tile_pool(name="keep", bufs=1))
+        psum = ctx.enter_context(tc.psum_pool(name="psum", bufs=1))
+
+        def sb(name, shape, dtype):
+            return keep.tile(shape, dtype, name=name, align_bytes=64)
+
+        def load_list(name, src):
+            lst = sb(name, [P, S // STRIPE], U16)
+            nc.sync.dma_start(lst[:], src)
+            return lst
+
+        def half_cols(u):
+            return slice(u * HALF, (u + 1) * HALF)
+
+        def half_offsets(lst, u):
+            return lst[:, u * HALF // STRIPE : (u + 1) * HALF // STRIPE]
+
+        def load_scale_rows(queue, plane, src):
+            for q in range(4):
+                queue.dma_start(plane[32 * q : 32 * q + 4, :].bitcast(I32), src[0, 4 * q : 4 * q + 4, :].bitcast(I32))
+
+        def words_view(src):
+            return src[0].rearrange("p n r -> p (n r)").bitcast(I32)
+
+        def woven(tile3):
+            return tile3[:].rearrange("p (c i) t -> p c t i", i=2)
+
+        def planar(tile3):
+            return tile3[:].rearrange("p t (c i) -> p c t i", i=2)
+
+        x_plane = sb("x_plane", [P, T], U8)
+        nc.vector.memset(x_plane[:].bitcast(I32), 0)
+        w1_plane = sb("w1_plane", [P, N], U8)
+        nc.gpsimd.memset(w1_plane[:].bitcast(I32), 0)
+
+        offs_sb = load_list("offs_sb", offs)
+        two_sb = load_list("two_sb", two)
+        load_scale_rows(nc.scalar, x_plane, x_scales)
+        x_codes = sb("x_codes", [P, T], U32)
+        nc.sync.dma_start(x_codes[:].bitcast(I32), words_view(x_words))
+        gt_sb = sb("gt_sb", [P, PACK], F32)
+        nc.gpsimd.dma_start(gt_sb[:], gt.rearrange("(p t) o -> p (t o)", t=PACK))
+        load_scale_rows(nc.gpsimd, w1_plane, w1_scales)
+
+        raw = {}
+
+        def load_weight(name, w):
+            rows = w.rearrange("(p t) c -> p t c", t=PACK)
+            for u in range(HALVES):
+                raw[name, u] = sb(f"{name}_raw{u}", [P, PACK, HALF], F32)
+                nc.sync.dma_start(raw[name, u][:], rows[:, :, half_cols(u)])
+
+        load_weight("wa", wa)
+        n1_sb = load_list("n1_sb", n1)
+        n2_sb = load_list("n2_sb", n2)
+        load_weight("wb", wb)
+        w1_codes = sb("w1_codes", [P, N], U32)
+        nc.sync.dma_start(w1_codes[:].bitcast(I32), words_view(w1_words))
+        n3_sb = load_list("n3_sb", n3)
+        n4_sb = load_list("n4_sb", n4)
+
+        picked_bytes = sb("picked_bytes", [P, 2, S], U8)
+        for s, lst in enumerate((offs_sb, two_sb)):
+            nc.vector.tensor_copy(picked_bytes[:, s, :], x_plane[:].indirect(lst[:]))
+        picked_plane = sb("picked_plane", [P, 2, S], U8)
+        nc.vector.tensor_copy(
+            picked_plane[:].rearrange("p s (t m) -> p s t m", t=PACK),
+            picked_bytes[:].rearrange("p s (m t) -> p s t m", t=PACK),
+        )
+        picked_codes = []
+        for s, lst in enumerate((offs_sb, two_sb)):
+            codes = sb(f"picked_codes{s}", [P, S], U32)
+            nc.vector.tensor_copy(codes[:].rearrange("p (t m) -> p m t", t=PACK), x_codes[:].indirect(lst[:]))
+            picked_codes.append(codes)
+
+        banks = {}
+        for s, name in enumerate(("wa", "wb")):
+            for t in range(PACK):
+                banks[s, t] = psum.tile([P, H], F32, name=f"first{s}{t}", tag=f"bank{s}{t}")
+            for u in range(HALVES):
+                rounded = sb(f"{name}_bf{u}", [P, HALF, PACK], BF16)
+                if (s, u) == (1, HALVES - 1):
+                    nc.vector.tensor_copy(woven(rounded), planar(raw[name, u]))
+                else:
+                    nc.scalar.copy(woven(rounded), planar(raw[name, u]))
+                w_codes = sb(f"{name}_codes{u}", [P, HALF], U32)
+                w_plane = sb(f"{name}_plane{u}", [P, HALF], U8)
+                nc.vector.quantize_mx(w_codes[:].bitcast(FP8X4), w_plane[:], rounded[:].rearrange("p c t -> p (c t)"))
+                for t in range(PACK):
+                    rows = slice(t * P, (t + 1) * P)
+                    nc.tensor.matmul_mx(
+                        banks[s, t][:, half_cols(u)],
+                        lhsT=picked_codes[s][:, rows].bitcast(FP8X4),
+                        lhsT_scale=picked_plane[:, s, rows],
+                        rhs=w_codes[:].bitcast(FP8X4),
+                        rhs_scale=w_plane[:],
+                        start=True,
+                        stop=True,
+                    )
+
+        w1_dealt = sb("w1_dealt", [P, N], U32)
+        nc.vector.tensor_copy(
+            w1_dealt[:].bitcast(I32).rearrange("p (t m) -> p m t", t=PACK),
+            w1_codes[:].bitcast(I32).rearrange("p (m t) -> p m t", t=PACK),
+        )
+        w1_dealt_plane = sb("w1_dealt_plane", [P, N], U8)
+        nc.vector.tensor_copy(
+            w1_dealt_plane[:].rearrange("p (t m) -> p t m", t=PACK),
+            w1_plane[:].rearrange("p (m t) -> p t m", t=PACK),
+        )
+
+        y_sb = [sb(f"y_sb{t}", [P, H], F32) for t in range(PACK)]
+        d_sb = [sb(f"d_sb{t}", [P, H], F32) for t in range(PACK)]
+        h_sb = [sb(f"h_sb{t}", [P, H], F32) for t in range(PACK)]
+        tanh_sb = [sb(f"tanh_sb{t}", [P, H], F32) for t in range(PACK)]
+        h_banks = {}
+        for u in range(HALVES):
+            cols = half_cols(u)
+            d_n2 = sb(f"d_n2_{u}", [P, PACK, HALF], F32)
+            left = sb(f"left{u}", [P, PACK, HALF], F32)
+            right = sb(f"right{u}", [P, PACK, HALF], F32)
+            for t in range(PACK):
+                if u == 0:
+                    nc.scalar.activation(y_sb[t][:], banks[0, t][:], ACT.Copy, scale=gt_sb[:, t : t + 1])
+                    nc.scalar.activation(d_sb[t][:], banks[1, t][:], ACT.Copy, scale=0.75)
+                nc.scalar.activation(d_n2[:, t, :], d_sb[t][:].indirect(half_offsets(n2_sb, u)), ACT.Copy)
+                nc.vector.tensor_tensor(
+                    right[:, t, :], y_sb[t][:].indirect(half_offsets(n1_sb, u)), d_sb[t][:, cols], ALU.mult
+                )
+                nc.vector.tensor_tensor(left[:, t, :], y_sb[t][:, cols], d_n2[:, t, :], ALU.mult)
+            z_bf = sb(f"z_bf{u}", [P, HALF, PACK], BF16)
+            nc.vector.tensor_tensor(woven(z_bf), planar(left), planar(right), ALU.subtract)
+            z_codes = sb(f"z_codes{u}", [P, HALF], U32)
+            z_plane = sb(f"z_plane{u}", [P, HALF], U8)
+            nc.vector.quantize_mx(z_codes[:].bitcast(FP8X4), z_plane[:], z_bf[:].rearrange("p c t -> p (c t)"))
+            for t in range(PACK):
+                rows = slice(t * P, (t + 1) * P)
+                h_banks[u, t] = psum.tile([P, HALF], F32, name=f"second{u}{t}", tag=f"bank{u}{t}")
+                nc.tensor.matmul_mx(
+                    h_banks[u, t][:],
+                    lhsT=w1_dealt[:, rows].bitcast(FP8X4),
+                    lhsT_scale=w1_dealt_plane[:, rows],
+                    rhs=z_codes[:].bitcast(FP8X4),
+                    rhs_scale=z_plane[:],
+                    start=True,
+                    stop=True,
+                )
+
+        for u in range(HALVES):
+            for t in range(PACK):
+                nc.scalar.activation(tanh_sb[t][:, half_cols(u)], h_banks[u, t][:], ACT.Tanh)
+                nc.scalar.copy(h_sb[t][:, half_cols(u)], h_banks[u, t][:])
+
+        out_rows = out_0.rearrange("(p t) c -> p t c", t=PACK)
+        out_words = words_view(out_1)
+        out_plane = sb("out_plane", [P, H], U8)
+        for u in range(HALVES):
+            cols = half_cols(u)
+            h_n3 = sb(f"h_n3_{u}", [P, PACK, HALF], F32)
+            gated = sb(f"gated{u}", [P, PACK, HALF], F32)
+            for t in range(PACK):
+                nc.scalar.activation(h_n3[:, t, :], h_sb[t][:].indirect(half_offsets(n3_sb, u)), ACT.Copy)
+                nc.vector.tensor_tensor(
+                    gated[:, t, :], tanh_sb[t][:].indirect(half_offsets(n4_sb, u)), h_sb[t][:, cols], ALU.mult
+                )
+            result = sb(f"result{u}", [P, PACK, HALF], F32)
+            nc.vector.tensor_tensor(result[:], gated[:], h_n3[:], ALU.mult)
+            nc.sync.dma_start(out_rows[:, :, cols], result[:])
+            out_bf = sb(f"out_bf{u}", [P, HALF, PACK], BF16)
+            nc.vector.tensor_copy(woven(out_bf), planar(result))
+            out_codes = sb(f"out_codes{u}", [P, HALF], U32)
+            nc.vector.quantize_mx(
+                out_codes[:].bitcast(FP8X4), out_plane[:, cols], out_bf[:].rearrange("p c t -> p (c t)")
+            )
+            nc.sync.dma_start(out_words[:, cols], out_codes[:].bitcast(I32))
+        for q in range(4):
+            queue = nc.scalar if q % 2 else nc.sync
+            queue.dma_start(
+                out_2[0, 4 * q : 4 * q + 4, :].bitcast(I32), out_plane[32 * q : 32 * q + 4, :].bitcast(I32)
+            )

@@ -20,6 +20,7 @@ PACK = 4
 HALF = 256
 HALVES = H // HALF
 STRIPE = 16
+FUSED = 2
 
 
 def tile_picked_twtcrossbcube_none_po_kernel(
@@ -28,6 +29,7 @@ def tile_picked_twtcrossbcube_none_po_kernel(
     nc = tc.nc
     with ExitStack() as ctx:
         keep = ctx.enter_context(tc.tile_pool(name="keep", bufs=1))
+        shared = ctx.enter_context(tc.tile_pool(name="shared", bufs=1))
         psum = ctx.enter_context(tc.psum_pool(name="psum", bufs=1))
 
         def sb(name, shape, dtype):
@@ -58,74 +60,81 @@ def tile_picked_twtcrossbcube_none_po_kernel(
             return tile3[:].rearrange("p t (c i) -> p c t i", i=2)
 
         x_plane = sb("x_plane", [P, T], U8)
-        nc.vector.memset(x_plane[:].bitcast(I32), 0)
+        nc.gpsimd.memset(x_plane[:].bitcast(I32), 0)
         w1_plane = sb("w1_plane", [P, N], U8)
         nc.gpsimd.memset(w1_plane[:].bitcast(I32), 0)
 
+        gt_sb = sb("gt_sb", [P, PACK], F32)
+        nc.scalar.dma_start(gt_sb[:], gt.rearrange("(p t) o -> p (t o)", t=PACK))
         offs_sb = load_list("offs_sb", offs)
-        two_sb = load_list("two_sb", two)
-        load_scale_rows(nc.scalar, x_plane, x_scales)
         x_codes = sb("x_codes", [P, T], U32)
         nc.sync.dma_start(x_codes[:].bitcast(I32), words_view(x_words))
-        gt_sb = sb("gt_sb", [P, PACK], F32)
-        nc.gpsimd.dma_start(gt_sb[:], gt.rearrange("(p t) o -> p (t o)", t=PACK))
-        load_scale_rows(nc.gpsimd, w1_plane, w1_scales)
+        load_scale_rows(nc.sync, x_plane, x_scales)
+        two_sb = load_list("two_sb", two)
 
-        raw = {}
-
-        def load_weight(name, w):
+        raw = {
+            "wa": sb("wa_raw", [P, HALVES, PACK, HALF], F32),
+            "wb": shared.tile([P, HALVES, PACK, HALF], F32, name="wb_raw", offset=0),
+        }
+        for name, w in (("wa", wa), ("wb", wb)):
             rows = w.rearrange("(p t) c -> p t c", t=PACK)
             for u in range(HALVES):
-                raw[name, u] = sb(f"{name}_raw{u}", [P, PACK, HALF], F32)
-                nc.sync.dma_start(raw[name, u][:], rows[:, :, half_cols(u)])
-
-        load_weight("wa", wa)
+                nc.sync.dma_start(raw[name][:, u], rows[:, :, half_cols(u)])
         n1_sb = load_list("n1_sb", n1)
         n2_sb = load_list("n2_sb", n2)
-        load_weight("wb", wb)
         w1_codes = sb("w1_codes", [P, N], U32)
         nc.sync.dma_start(w1_codes[:].bitcast(I32), words_view(w1_words))
-        n3_sb = load_list("n3_sb", n3)
+        load_scale_rows(nc.sync, w1_plane, w1_scales)
         n4_sb = load_list("n4_sb", n4)
+        n3_sb = load_list("n3_sb", n3)
 
-        picked_bytes = sb("picked_bytes", [P, 2, S], U8)
+        gain = sb("gain", [P, PACK], F32)
+        nc.scalar.activation(gain[:], gt_sb[:], ACT.Copy, scale=0.75)
+
+        def pick_words(name, lst, tag):
+            codes = keep.tile([P, S], U32, name=name, tag=tag, align_bytes=64)
+            nc.vector.tensor_copy(codes[:].rearrange("p (t m) -> p m t", t=PACK), x_codes[:].indirect(lst[:]))
+            return codes
+
+        def quantize_weight(name):
+            rounded = sb(f"{name}_bf", [P, H, PACK], BF16)
+            for u in range(HALVES):
+                nc.scalar.copy(
+                    rounded[:, half_cols(u), :].rearrange("p (c i) t -> p c t i", i=2),
+                    raw[name][:, u].rearrange("p t (c i) -> p c t i", i=2),
+                )
+            w_codes = sb(f"{name}_codes", [P, H], U32)
+            w_plane = sb(f"{name}_plane", [P, H], U8)
+            nc.vector.quantize_mx(w_codes[:].bitcast(FP8X4), w_plane[:], rounded[:].rearrange("p c t -> p (c t)"))
+            return w_codes, w_plane
+
+        def first_product(s, codes, w_codes, w_plane):
+            banks = [psum.tile([P, H], F32, name=f"first{s}{t}", tag=f"bank{s}{t}") for t in range(PACK)]
+            for t in range(PACK):
+                rows = slice(t * P, (t + 1) * P)
+                nc.tensor.matmul_mx(
+                    banks[t][:],
+                    lhsT=codes[:, rows].bitcast(FP8X4),
+                    lhsT_scale=picked_plane[:, s, rows],
+                    rhs=w_codes[:].bitcast(FP8X4),
+                    rhs_scale=w_plane[:],
+                    start=True,
+                    stop=True,
+                )
+            return banks
+
+        offs_codes = pick_words("offs_codes", offs_sb, "offs_codes")
+        listed = sb("listed", [P, 2, S], U8)
         for s, lst in enumerate((offs_sb, two_sb)):
-            nc.vector.tensor_copy(picked_bytes[:, s, :], x_plane[:].indirect(lst[:]))
+            nc.vector.tensor_copy(listed[:, s, :], x_plane[:].indirect(lst[:]))
         picked_plane = sb("picked_plane", [P, 2, S], U8)
         nc.vector.tensor_copy(
             picked_plane[:].rearrange("p s (t m) -> p s t m", t=PACK),
-            picked_bytes[:].rearrange("p s (m t) -> p s t m", t=PACK),
+            listed[:].rearrange("p s (m t) -> p s t m", t=PACK),
         )
-        picked_codes = []
-        for s, lst in enumerate((offs_sb, two_sb)):
-            codes = sb(f"picked_codes{s}", [P, S], U32)
-            nc.vector.tensor_copy(codes[:].rearrange("p (t m) -> p m t", t=PACK), x_codes[:].indirect(lst[:]))
-            picked_codes.append(codes)
-
-        banks = {}
-        for s, name in enumerate(("wa", "wb")):
-            for t in range(PACK):
-                banks[s, t] = psum.tile([P, H], F32, name=f"first{s}{t}", tag=f"bank{s}{t}")
-            for u in range(HALVES):
-                rounded = sb(f"{name}_bf{u}", [P, HALF, PACK], BF16)
-                if (s, u) == (1, HALVES - 1):
-                    nc.vector.tensor_copy(woven(rounded), planar(raw[name, u]))
-                else:
-                    nc.scalar.copy(woven(rounded), planar(raw[name, u]))
-                w_codes = sb(f"{name}_codes{u}", [P, HALF], U32)
-                w_plane = sb(f"{name}_plane{u}", [P, HALF], U8)
-                nc.vector.quantize_mx(w_codes[:].bitcast(FP8X4), w_plane[:], rounded[:].rearrange("p c t -> p (c t)"))
-                for t in range(PACK):
-                    rows = slice(t * P, (t + 1) * P)
-                    nc.tensor.matmul_mx(
-                        banks[s, t][:, half_cols(u)],
-                        lhsT=picked_codes[s][:, rows].bitcast(FP8X4),
-                        lhsT_scale=picked_plane[:, s, rows],
-                        rhs=w_codes[:].bitcast(FP8X4),
-                        rhs_scale=w_plane[:],
-                        start=True,
-                        stop=True,
-                    )
+        y_banks = first_product(0, offs_codes, *quantize_weight("wa"))
+        two_codes = pick_words("two_codes", two_sb, "wa_bf")
+        d_banks = first_product(1, two_codes, *quantize_weight("wb"))
 
         w1_dealt = sb("w1_dealt", [P, N], U32)
         nc.vector.tensor_copy(
@@ -134,39 +143,47 @@ def tile_picked_twtcrossbcube_none_po_kernel(
         )
         w1_dealt_plane = sb("w1_dealt_plane", [P, N], U8)
         nc.vector.tensor_copy(
-            w1_dealt_plane[:].rearrange("p (t m) -> p t m", t=PACK),
-            w1_plane[:].rearrange("p (m t) -> p t m", t=PACK),
+            w1_dealt_plane[:].rearrange("p (t m) -> p t m", t=PACK), w1_plane[:].rearrange("p (m t) -> p t m", t=PACK)
         )
 
-        y_sb = [sb(f"y_sb{t}", [P, H], F32) for t in range(PACK)]
-        d_sb = [sb(f"d_sb{t}", [P, H], F32) for t in range(PACK)]
-        h_sb = [sb(f"h_sb{t}", [P, H], F32) for t in range(PACK)]
-        tanh_sb = [sb(f"tanh_sb{t}", [P, H], F32) for t in range(PACK)]
+        y_sb = [shared.tile([P, H], F32, name=f"y_sb{t}", offset=t * H * 4) for t in range(PACK)]
+        tanh_and_d = [sb(f"tanh_and_d{t}", [P, 2 * H], F32) for t in range(PACK)]
+        h_and_dn2 = [sb(f"h_and_dn2{t}", [P, 2 * H], F32) for t in range(PACK)]
+        d_sb = [both[:, H:] for both in tanh_and_d]
+        d_n2 = [both[:, H:] for both in h_and_dn2]
+        left = [sb(f"left{u}", [P, PACK, HALF], F32) for u in range(HALVES)]
+        right = [sb(f"right{u}", [P, PACK, HALF], F32) for u in range(HALVES)]
+        z_bf = [sb(f"z_bf{u}", [P, HALF, PACK], BF16) for u in range(HALVES)]
         h_banks = {}
-        for u in range(HALVES):
-            cols = half_cols(u)
-            d_n2 = sb(f"d_n2_{u}", [P, PACK, HALF], F32)
-            left = sb(f"left{u}", [P, PACK, HALF], F32)
-            right = sb(f"right{u}", [P, PACK, HALF], F32)
-            for t in range(PACK):
-                if u == 0:
-                    nc.scalar.activation(y_sb[t][:], banks[0, t][:], ACT.Copy, scale=gt_sb[:, t : t + 1])
-                    nc.scalar.activation(d_sb[t][:], banks[1, t][:], ACT.Copy, scale=0.75)
-                nc.scalar.activation(d_n2[:, t, :], d_sb[t][:].indirect(half_offsets(n2_sb, u)), ACT.Copy)
-                nc.vector.tensor_tensor(
-                    right[:, t, :], y_sb[t][:].indirect(half_offsets(n1_sb, u)), d_sb[t][:, cols], ALU.mult
-                )
-                nc.vector.tensor_tensor(left[:, t, :], y_sb[t][:, cols], d_n2[:, t, :], ALU.mult)
-            z_bf = sb(f"z_bf{u}", [P, HALF, PACK], BF16)
-            nc.vector.tensor_tensor(woven(z_bf), planar(left), planar(right), ALU.subtract)
+
+        def fetch_d(t, u):
+            nc.scalar.activation(d_n2[t][:, half_cols(u)], d_sb[t].indirect(half_offsets(n2_sb, u)), ACT.Copy)
+
+        def right_term(t, u):
+            nc.vector.tensor_tensor(
+                right[u][:, t, :], y_sb[t][:].indirect(half_offsets(n1_sb, u)), d_sb[t][:, half_cols(u)], ALU.mult
+            )
+
+        def right_term_shared(t, u):
+            y_n1 = sb(f"y_n1_{t}", [P, HALF], F32)
+            nc.scalar.activation(y_n1[:], y_sb[t][:].indirect(half_offsets(n1_sb, u)), ACT.Copy)
+            nc.vector.tensor_tensor(right[u][:, t, :], y_n1[:], d_sb[t][:, half_cols(u)], ALU.mult)
+
+        def left_term(t, u):
+            nc.vector.tensor_tensor(left[u][:, t, :], y_sb[t][:, half_cols(u)], d_n2[t][:, half_cols(u)], ALU.mult)
+
+        def subtract(u):
+            nc.vector.tensor_tensor(woven(z_bf[u]), planar(left[u]), planar(right[u]), ALU.subtract)
+
+        def second_product(u):
             z_codes = sb(f"z_codes{u}", [P, HALF], U32)
             z_plane = sb(f"z_plane{u}", [P, HALF], U8)
-            nc.vector.quantize_mx(z_codes[:].bitcast(FP8X4), z_plane[:], z_bf[:].rearrange("p c t -> p (c t)"))
+            nc.vector.quantize_mx(z_codes[:].bitcast(FP8X4), z_plane[:], z_bf[u][:].rearrange("p c t -> p (c t)"))
             for t in range(PACK):
                 rows = slice(t * P, (t + 1) * P)
-                h_banks[u, t] = psum.tile([P, HALF], F32, name=f"second{u}{t}", tag=f"bank{u}{t}")
+                h_banks[t, u] = psum.tile([P, HALF], F32, name=f"second{u}{t}", tag=f"bank{u}{t}")
                 nc.tensor.matmul_mx(
-                    h_banks[u, t][:],
+                    h_banks[t, u][:],
                     lhsT=w1_dealt[:, rows].bitcast(FP8X4),
                     lhsT_scale=w1_dealt_plane[:, rows],
                     rhs=z_codes[:].bitcast(FP8X4),
@@ -175,28 +192,70 @@ def tile_picked_twtcrossbcube_none_po_kernel(
                     stop=True,
                 )
 
-        for u in range(HALVES):
-            for t in range(PACK):
-                nc.scalar.activation(tanh_sb[t][:, half_cols(u)], h_banks[u, t][:], ACT.Tanh)
-                nc.scalar.copy(h_sb[t][:, half_cols(u)], h_banks[u, t][:])
+        def tanh_out(t, u):
+            nc.scalar.activation(tanh_and_d[t][:, half_cols(u)], h_banks[t, u][:], ACT.Tanh)
+
+        def h_out(t, u):
+            nc.scalar.copy(h_and_dn2[t][:, half_cols(u)], h_banks[t, u][:])
+
+        for t in range(PACK):
+            nc.scalar.activation(y_sb[t][:], y_banks[t][:], ACT.Copy, scale=gain[:, t : t + 1])
+            if t == 0:
+                nc.vector.tensor_copy(d_sb[t], d_banks[t][:])
+            else:
+                nc.scalar.copy(d_sb[t], d_banks[t][:])
+            fetch_d(t, 0)
+            right_term(t, 0)
+            if t < FUSED:
+                right_term(t, 1)
+            left_term(t, 0)
+        for t in range(PACK):
+            fetch_d(t, 1)
+        left_term(0, 1)
+        subtract(0)
+        left_term(1, 1)
+        second_product(0)
+        for t in range(2, PACK):
+            left_term(t, 1)
+        for t in range(FUSED, PACK):
+            right_term_shared(t, 1)
+        for t in range(PACK):
+            tanh_out(t, 0)
+            h_out(t, 0)
+        subtract(1)
+        second_product(1)
 
         out_rows = out_0.rearrange("(p t) c -> p t c", t=PACK)
         out_words = words_view(out_1)
         out_plane = sb("out_plane", [P, H], U8)
+        h_n3 = [sb(f"h_n3_{t}", [P, H], F32) for t in range(PACK)]
+        gated = [sb(f"gated{t}", [P, H], F32) for t in range(PACK)]
+        result = sb("result", [P, PACK, H], F32)
+
+        def finish(t):
+            nc.scalar.activation(h_n3[t][:], h_and_dn2[t][:].indirect(n3_sb[:]), ACT.Copy)
+            nc.vector.tensor_tensor(result[:, t, :], gated[t][:], h_n3[t][:], ALU.mult)
+            nc.sync.dma_start(out_rows[:, t, :], result[:, t, :])
+
+        for t in range(PACK):
+            tanh_out(t, 1)
+            if t == 0:
+                nc.vector.tensor_copy(h_and_dn2[t][:, half_cols(1)], h_banks[t, 1][:])
+            else:
+                h_out(t, 1)
+            nc.vector.tensor_tensor(gated[t][:], tanh_and_d[t][:].indirect(n4_sb[:]), h_and_dn2[t][:, :H], ALU.mult)
+            if t > 0:
+                finish(t - 1)
+        finish(PACK - 1)
+
         for u in range(HALVES):
             cols = half_cols(u)
-            h_n3 = sb(f"h_n3_{u}", [P, PACK, HALF], F32)
-            gated = sb(f"gated{u}", [P, PACK, HALF], F32)
-            for t in range(PACK):
-                nc.scalar.activation(h_n3[:, t, :], h_sb[t][:].indirect(half_offsets(n3_sb, u)), ACT.Copy)
-                nc.vector.tensor_tensor(
-                    gated[:, t, :], tanh_sb[t][:].indirect(half_offsets(n4_sb, u)), h_sb[t][:, cols], ALU.mult
-                )
-            result = sb(f"result{u}", [P, PACK, HALF], F32)
-            nc.vector.tensor_tensor(result[:], gated[:], h_n3[:], ALU.mult)
-            nc.sync.dma_start(out_rows[:, :, cols], result[:])
             out_bf = sb(f"out_bf{u}", [P, HALF, PACK], BF16)
-            nc.vector.tensor_copy(woven(out_bf), planar(result))
+            source = result[:, :, cols].rearrange("p t (c i) -> p c t i", i=2)
+            if u == 0:
+                nc.vector.tensor_copy(woven(out_bf), source)
+            else:
+                nc.scalar.copy(woven(out_bf), source)
             out_codes = sb(f"out_codes{u}", [P, HALF], U32)
             nc.vector.quantize_mx(
                 out_codes[:].bitcast(FP8X4), out_plane[:, cols], out_bf[:].rearrange("p c t -> p (c t)")

@@ -20,7 +20,7 @@ PACK = 4
 HALF = 256
 HALVES = H // HALF
 STRIPE = 16
-FUSED = 2
+FUSED = 3
 
 
 def tile_picked_twtcrossbcube_none_po_kernel(
@@ -64,8 +64,6 @@ def tile_picked_twtcrossbcube_none_po_kernel(
         w1_plane = sb("w1_plane", [P, N], U8)
         nc.gpsimd.memset(w1_plane[:].bitcast(I32), 0)
 
-        gt_sb = sb("gt_sb", [P, PACK], F32)
-        nc.scalar.dma_start(gt_sb[:], gt.rearrange("(p t) o -> p (t o)", t=PACK))
         offs_sb = load_list("offs_sb", offs)
         x_codes = sb("x_codes", [P, T], U32)
         nc.sync.dma_start(x_codes[:].bitcast(I32), words_view(x_words))
@@ -80,6 +78,8 @@ def tile_picked_twtcrossbcube_none_po_kernel(
             rows = w.rearrange("(p t) c -> p t c", t=PACK)
             for u in range(HALVES):
                 nc.sync.dma_start(raw[name][:, u], rows[:, :, half_cols(u)])
+        gt_sb = sb("gt_sb", [P, PACK], F32)
+        nc.sync.dma_start(gt_sb[:], gt.rearrange("(p t) o -> p (t o)", t=PACK))
         n1_sb = load_list("n1_sb", n1)
         n2_sb = load_list("n2_sb", n2)
         w1_codes = sb("w1_codes", [P, N], U32)
@@ -87,9 +87,6 @@ def tile_picked_twtcrossbcube_none_po_kernel(
         load_scale_rows(nc.sync, w1_plane, w1_scales)
         n4_sb = load_list("n4_sb", n4)
         n3_sb = load_list("n3_sb", n3)
-
-        gain = sb("gain", [P, PACK], F32)
-        nc.scalar.activation(gain[:], gt_sb[:], ACT.Copy, scale=0.75)
 
         def pick_words(name, lst, tag):
             codes = keep.tile([P, S], U32, name=name, tag=tag, align_bytes=64)
@@ -99,29 +96,29 @@ def tile_picked_twtcrossbcube_none_po_kernel(
         def quantize_weight(name):
             rounded = sb(f"{name}_bf", [P, H, PACK], BF16)
             for u in range(HALVES):
-                nc.scalar.copy(
+                nc.scalar.activation(
                     rounded[:, half_cols(u), :].rearrange("p (c i) t -> p c t i", i=2),
                     raw[name][:, u].rearrange("p t (c i) -> p c t i", i=2),
+                    ACT.Copy,
                 )
             w_codes = sb(f"{name}_codes", [P, H], U32)
             w_plane = sb(f"{name}_plane", [P, H], U8)
             nc.vector.quantize_mx(w_codes[:].bitcast(FP8X4), w_plane[:], rounded[:].rearrange("p c t -> p (c t)"))
             return w_codes, w_plane
 
-        def first_product(s, codes, w_codes, w_plane):
-            banks = [psum.tile([P, H], F32, name=f"first{s}{t}", tag=f"bank{s}{t}") for t in range(PACK)]
-            for t in range(PACK):
-                rows = slice(t * P, (t + 1) * P)
-                nc.tensor.matmul_mx(
-                    banks[t][:],
-                    lhsT=codes[:, rows].bitcast(FP8X4),
-                    lhsT_scale=picked_plane[:, s, rows],
-                    rhs=w_codes[:].bitcast(FP8X4),
-                    rhs_scale=w_plane[:],
-                    start=True,
-                    stop=True,
-                )
-            return banks
+        def first_product(s, t, codes, w_mx, tag):
+            bank = psum.tile([P, H], F32, name=f"first{s}{t}", tag=tag)
+            rows = slice(t * P, (t + 1) * P)
+            nc.tensor.matmul_mx(
+                bank[:],
+                lhsT=codes[:, rows].bitcast(FP8X4),
+                lhsT_scale=picked_plane[:, s, rows],
+                rhs=w_mx[0][:].bitcast(FP8X4),
+                rhs_scale=w_mx[1][:],
+                start=True,
+                stop=True,
+            )
+            return bank
 
         offs_codes = pick_words("offs_codes", offs_sb, "offs_codes")
         listed = sb("listed", [P, 2, S], U8)
@@ -132,9 +129,11 @@ def tile_picked_twtcrossbcube_none_po_kernel(
             picked_plane[:].rearrange("p s (t m) -> p s t m", t=PACK),
             listed[:].rearrange("p s (m t) -> p s t m", t=PACK),
         )
-        y_banks = first_product(0, offs_codes, *quantize_weight("wa"))
+        wa_mx = quantize_weight("wa")
+        y_banks = [first_product(0, t, offs_codes, wa_mx, f"bank0{t}") for t in range(PACK - 1)]
         two_codes = pick_words("two_codes", two_sb, "wa_bf")
-        d_banks = first_product(1, two_codes, *quantize_weight("wb"))
+        wb_mx = quantize_weight("wb")
+        d_banks = [first_product(1, t, two_codes, wb_mx, f"bank1{t}") for t in range(PACK)]
 
         w1_dealt = sb("w1_dealt", [P, N], U32)
         nc.vector.tensor_copy(
@@ -181,7 +180,7 @@ def tile_picked_twtcrossbcube_none_po_kernel(
             nc.vector.quantize_mx(z_codes[:].bitcast(FP8X4), z_plane[:], z_bf[u][:].rearrange("p c t -> p (c t)"))
             for t in range(PACK):
                 rows = slice(t * P, (t + 1) * P)
-                h_banks[t, u] = psum.tile([P, HALF], F32, name=f"second{u}{t}", tag=f"bank{u}{t}")
+                h_banks[t, u] = psum.tile([P, HALF], F32, name=f"second{u}{t}", tag=f"bank{u}{(t + 1) % PACK}")
                 nc.tensor.matmul_mx(
                     h_banks[t, u][:],
                     lhsT=w1_dealt[:, rows].bitcast(FP8X4),
@@ -199,11 +198,12 @@ def tile_picked_twtcrossbcube_none_po_kernel(
             nc.scalar.copy(h_and_dn2[t][:, half_cols(u)], h_banks[t, u][:])
 
         for t in range(PACK):
-            nc.scalar.activation(y_sb[t][:], y_banks[t][:], ACT.Copy, scale=gain[:, t : t + 1])
+            nc.scalar.activation(y_sb[t][:], y_banks[t][:], ACT.Copy, scale=gt_sb[:, t : t + 1])
             if t == 0:
-                nc.vector.tensor_copy(d_sb[t], d_banks[t][:])
+                y_banks.append(first_product(0, PACK - 1, offs_codes, wa_mx, "bank00"))
+                nc.vector.tensor_scalar_mul(d_sb[t], d_banks[t][:], 0.75)
             else:
-                nc.scalar.copy(d_sb[t], d_banks[t][:])
+                nc.scalar.activation(d_sb[t], d_banks[t][:], ACT.Copy, scale=0.75)
             fetch_d(t, 0)
             right_term(t, 0)
             if t < FUSED:
@@ -228,37 +228,48 @@ def tile_picked_twtcrossbcube_none_po_kernel(
         out_rows = out_0.rearrange("(p t) c -> p t c", t=PACK)
         out_words = words_view(out_1)
         out_plane = sb("out_plane", [P, H], U8)
-        h_n3 = [sb(f"h_n3_{t}", [P, H], F32) for t in range(PACK)]
+        h_n3 = [sb(f"h_n3_{u}", [P, PACK, HALF], F32) for u in range(HALVES)]
         gated = [sb(f"gated{t}", [P, H], F32) for t in range(PACK)]
-        result = sb("result", [P, PACK, H], F32)
+        result = [sb(f"result{u}", [P, PACK, HALF], F32) for u in range(HALVES)]
 
-        def finish(t):
-            nc.scalar.activation(h_n3[t][:], h_and_dn2[t][:].indirect(n3_sb[:]), ACT.Copy)
-            nc.vector.tensor_tensor(result[:, t, :], gated[t][:], h_n3[t][:], ALU.mult)
-            nc.sync.dma_start(out_rows[:, t, :], result[:, t, :])
+        def finish(t, u):
+            nc.scalar.activation(h_n3[u][:, t, :], h_and_dn2[t][:].indirect(half_offsets(n3_sb, u)), ACT.Copy)
+            nc.vector.tensor_tensor(result[u][:, t, :], gated[t][:, half_cols(u)], h_n3[u][:, t, :], ALU.mult)
 
+        tanh_out(0, 1)
+        h_out(0, 1)
         for t in range(PACK):
-            tanh_out(t, 1)
             if t == 0:
-                nc.vector.tensor_copy(h_and_dn2[t][:, half_cols(1)], h_banks[t, 1][:])
+                for u in range(HALVES):
+                    nc.vector.tensor_tensor(
+                        gated[t][:, half_cols(u)],
+                        tanh_and_d[t][:].indirect(half_offsets(n4_sb, u)),
+                        h_and_dn2[t][:, half_cols(u)],
+                        ALU.mult,
+                    )
             else:
-                h_out(t, 1)
-            nc.vector.tensor_tensor(gated[t][:], tanh_and_d[t][:].indirect(n4_sb[:]), h_and_dn2[t][:, :H], ALU.mult)
+                nc.vector.tensor_tensor(
+                    gated[t][:], tanh_and_d[t][:].indirect(n4_sb[:]), h_and_dn2[t][:, :H], ALU.mult
+                )
+            if t + 1 < PACK:
+                tanh_out(t + 1, 1)
+                h_out(t + 1, 1)
             if t > 0:
-                finish(t - 1)
-        finish(PACK - 1)
+                finish(t - 1, 0)
+        finish(PACK - 1, 0)
+        nc.sync.dma_start(out_rows[:, :, half_cols(0)], result[0][:])
+        for t in range(PACK):
+            finish(t, 1)
+        nc.sync.dma_start(out_rows[:, :, half_cols(1)], result[1][:])
 
-        for u in range(HALVES):
+        out_bf = [sb(f"out_bf{u}", [P, HALF, PACK], BF16) for u in range(HALVES)]
+        nc.scalar.copy(woven(out_bf[0]), planar(result[0]))
+        nc.vector.tensor_copy(woven(out_bf[1]), planar(result[1]))
+        for u in reversed(range(HALVES)):
             cols = half_cols(u)
-            out_bf = sb(f"out_bf{u}", [P, HALF, PACK], BF16)
-            source = result[:, :, cols].rearrange("p t (c i) -> p c t i", i=2)
-            if u == 0:
-                nc.vector.tensor_copy(woven(out_bf), source)
-            else:
-                nc.scalar.copy(woven(out_bf), source)
             out_codes = sb(f"out_codes{u}", [P, HALF], U32)
             nc.vector.quantize_mx(
-                out_codes[:].bitcast(FP8X4), out_plane[:, cols], out_bf[:].rearrange("p c t -> p (c t)")
+                out_codes[:].bitcast(FP8X4), out_plane[:, cols], out_bf[u][:].rearrange("p c t -> p (c t)")
             )
             nc.sync.dma_start(out_words[:, cols], out_codes[:].bitcast(I32))
         for q in range(4):

from contextlib import ExitStack

import concourse.mybir as mybir

K, T, S, N, H = 512, 2048, 512, 512, 512
FLOPS = 2 * K * S * H * 2 + 2 * S * N * H

F32 = mybir.dt.float32
BF16 = mybir.dt.bfloat16
I32 = mybir.dt.int32
U32 = mybir.dt.uint32
U16 = mybir.dt.uint16
U8 = mybir.dt.uint8
FP8X4 = mybir.dt.float8_e4m3fn_x4
ALU = mybir.AluOpType
ACT = mybir.ActivationFunctionType

P = 128
PACK = 4
HALF = 256
HALVES = H // HALF
STRIPE = 16
FUSED = 3


def tile_picked_twtcrossbcube_none_po_kernel(
    tc, x_words, x_scales, wa, wb, gt, w1_words, w1_scales, offs, two, n1, n2, n3, n4, out_0, out_1, out_2
):
    nc = tc.nc
    with ExitStack() as ctx:
        keep = ctx.enter_context(tc.tile_pool(name="keep", bufs=1))
        shared = ctx.enter_context(tc.tile_pool(name="shared", bufs=1))
        psum = ctx.enter_context(tc.psum_pool(name="psum", bufs=1))

        def sb(name, shape, dtype):
            return keep.tile(shape, dtype, name=name, align_bytes=64)

        def load_list(name, src):
            lst = sb(name, [P, S // STRIPE], U16)
            nc.sync.dma_start(lst[:], src)
            return lst

        def half_cols(u):
            return slice(u * HALF, (u + 1) * HALF)

        def half_offsets(lst, u):
            return lst[:, u * HALF // STRIPE : (u + 1) * HALF // STRIPE]

        def load_scale_rows(queue, plane, src):
            for q in range(4):
                queue.dma_start(plane[32 * q : 32 * q + 4, :].bitcast(I32), src[0, 4 * q : 4 * q + 4, :].bitcast(I32))

        def words_view(src):
            return src[0].rearrange("p n r -> p (n r)").bitcast(I32)

        def woven(tile3):
            return tile3[:].rearrange("p (c i) t -> p c t i", i=2)

        def planar(tile3):
            return tile3[:].rearrange("p t (c i) -> p c t i", i=2)

        x_plane = sb("x_plane", [P, T], U8)
        nc.gpsimd.memset(x_plane[:].bitcast(I32), 0)
        w1_plane = sb("w1_plane", [P, N], U8)
        nc.gpsimd.memset(w1_plane[:].bitcast(I32), 0)

        offs_sb = load_list("offs_sb", offs)
        x_codes = sb("x_codes", [P, T], U32)
        nc.sync.dma_start(x_codes[:].bitcast(I32), words_view(x_words))
        load_scale_rows(nc.sync, x_plane, x_scales)
        two_sb = load_list("two_sb", two)

        raw = {
            "wa": sb("wa_raw", [P, HALVES, PACK, HALF], F32),
            "wb": shared.tile([P, HALVES, PACK, HALF], F32, name="wb_raw", offset=0),
        }
        for name, w in (("wa", wa), ("wb", wb)):
            rows = w.rearrange("(p t) c -> p t c", t=PACK)
            for u in range(HALVES):
                nc.sync.dma_start(raw[name][:, u], rows[:, :, half_cols(u)])
        gt_sb = sb("gt_sb", [P, PACK], F32)
        nc.sync.dma_start(gt_sb[:], gt.rearrange("(p t) o -> p (t o)", t=PACK))
        n1_sb = load_list("n1_sb", n1)
        n2_sb = load_list("n2_sb", n2)
        w1_codes = sb("w1_codes", [P, N], U32)
        nc.sync.dma_start(w1_codes[:].bitcast(I32), words_view(w1_words))
        load_scale_rows(nc.sync, w1_plane, w1_scales)
        n4_sb = load_list("n4_sb", n4)
        n3_sb = load_list("n3_sb", n3)

        def pick_words(name, lst, tag):
            codes = keep.tile([P, S], U32, name=name, tag=tag, align_bytes=64)
            nc.vector.tensor_copy(codes[:].rearrange("p (t m) -> p m t", t=PACK), x_codes[:].indirect(lst[:]))
            return codes

        def quantize_weight(name):
            rounded = sb(f"{name}_bf", [P, H, PACK], BF16)
            for u in range(HALVES):
                nc.scalar.activation(
                    rounded[:, half_cols(u), :].rearrange("p (c i) t -> p c t i", i=2),
                    raw[name][:, u].rearrange("p t (c i) -> p c t i", i=2),
                    ACT.Copy,
                )
            w_codes = sb(f"{name}_codes", [P, H], U32)
            w_plane = sb(f"{name}_plane", [P, H], U8)
            nc.vector.quantize_mx(w_codes[:].bitcast(FP8X4), w_plane[:], rounded[:].rearrange("p c t -> p (c t)"))
            return w_codes, w_plane

        def first_product(s, t, codes, w_mx, tag):
            bank = psum.tile([P, H], F32, name=f"first{s}{t}", tag=tag)
            rows = slice(t * P, (t + 1) * P)
            nc.tensor.matmul_mx(
                bank[:],
                lhsT=codes[:, rows].bitcast(FP8X4),
                lhsT_scale=picked_plane[:, s, rows],
                rhs=w_mx[0][:].bitcast(FP8X4),
                rhs_scale=w_mx[1][:],
                start=True,
                stop=True,
            )
            return bank

        offs_codes = pick_words("offs_codes", offs_sb, "offs_codes")
        listed = sb("listed", [P, 2, S], U8)
        for s, lst in enumerate((offs_sb, two_sb)):
            nc.vector.tensor_copy(listed[:, s, :], x_plane[:].indirect(lst[:]))
        picked_plane = sb("picked_plane", [P, 2, S], U8)
        nc.vector.tensor_copy(
            picked_plane[:].rearrange("p s (t m) -> p s t m", t=PACK),
            listed[:].rearrange("p s (m t) -> p s t m", t=PACK),
        )
        wa_mx = quantize_weight("wa")
        y_banks = [first_product(0, t, offs_codes, wa_mx, f"bank0{t}") for t in range(PACK - 1)]
        two_codes = pick_words("two_codes", two_sb, "wa_bf")
        wb_mx = quantize_weight("wb")
        d_banks = [first_product(1, t, two_codes, wb_mx, f"bank1{t}") for t in range(PACK)]

        w1_dealt = sb("w1_dealt", [P, N], U32)
        nc.vector.tensor_copy(
            w1_dealt[:].bitcast(I32).rearrange("p (t m) -> p m t", t=PACK),
            w1_codes[:].bitcast(I32).rearrange("p (m t) -> p m t", t=PACK),
        )
        w1_dealt_plane = sb("w1_dealt_plane", [P, N], U8)
        nc.vector.tensor_copy(
            w1_dealt_plane[:].rearrange("p (t m) -> p t m", t=PACK), w1_plane[:].rearrange("p (m t) -> p t m", t=PACK)
        )

        y_sb = [shared.tile([P, H], F32, name=f"y_sb{t}", offset=t * H * 4) for t in range(PACK)]
        tanh_and_d = [sb(f"tanh_and_d{t}", [P, 2 * H], F32) for t in range(PACK)]
        h_and_dn2 = [sb(f"h_and_dn2{t}", [P, 2 * H], F32) for t in range(PACK)]
        d_sb = [both[:, H:] for both in tanh_and_d]
        d_n2 = [both[:, H:] for both in h_and_dn2]
        left = [sb(f"left{u}", [P, PACK, HALF], F32) for u in range(HALVES)]
        right = [sb(f"right{u}", [P, PACK, HALF], F32) for u in range(HALVES)]
        z_bf = [sb(f"z_bf{u}", [P, HALF, PACK], BF16) for u in range(HALVES)]
        h_banks = {}

        def fetch_d(t, u):
            nc.scalar.activation(d_n2[t][:, half_cols(u)], d_sb[t].indirect(half_offsets(n2_sb, u)), ACT.Copy)

        def right_term(t, u):
            nc.vector.tensor_tensor(
                right[u][:, t, :], y_sb[t][:].indirect(half_offsets(n1_sb, u)), d_sb[t][:, half_cols(u)], ALU.mult
            )

        def right_term_shared(t, u):
            y_n1 = sb(f"y_n1_{t}", [P, HALF], F32)
            nc.scalar.activation(y_n1[:], y_sb[t][:].indirect(half_offsets(n1_sb, u)), ACT.Copy)
            nc.vector.tensor_tensor(right[u][:, t, :], y_n1[:], d_sb[t][:, half_cols(u)], ALU.mult)

        def left_term(t, u):
            nc.vector.tensor_tensor(left[u][:, t, :], y_sb[t][:, half_cols(u)], d_n2[t][:, half_cols(u)], ALU.mult)

        def subtract(u):
            nc.vector.tensor_tensor(woven(z_bf[u]), planar(left[u]), planar(right[u]), ALU.subtract)

        def second_product(u):
            z_codes = sb(f"z_codes{u}", [P, HALF], U32)
            z_plane = sb(f"z_plane{u}", [P, HALF], U8)
            nc.vector.quantize_mx(z_codes[:].bitcast(FP8X4), z_plane[:], z_bf[u][:].rearrange("p c t -> p (c t)"))
            for t in range(PACK):
                rows = slice(t * P, (t + 1) * P)
                h_banks[t, u] = psum.tile([P, HALF], F32, name=f"second{u}{t}", tag=f"bank{u}{(t + 1) % PACK}")
                nc.tensor.matmul_mx(
                    h_banks[t, u][:],
                    lhsT=w1_dealt[:, rows].bitcast(FP8X4),
                    lhsT_scale=w1_dealt_plane[:, rows],
                    rhs=z_codes[:].bitcast(FP8X4),
                    rhs_scale=z_plane[:],
                    start=True,
                    stop=True,
                )

        def tanh_out(t, u):
            nc.scalar.activation(tanh_and_d[t][:, half_cols(u)], h_banks[t, u][:], ACT.Tanh)

        def h_out(t, u):
            nc.scalar.copy(h_and_dn2[t][:, half_cols(u)], h_banks[t, u][:])

        for t in range(PACK):
            nc.scalar.activation(y_sb[t][:], y_banks[t][:], ACT.Copy, scale=gt_sb[:, t : t + 1])
            if t == 0:
                y_banks.append(first_product(0, PACK - 1, offs_codes, wa_mx, "bank00"))
                nc.vector.tensor_scalar_mul(d_sb[t], d_banks[t][:], 0.75)
            else:
                nc.scalar.activation(d_sb[t], d_banks[t][:], ACT.Copy, scale=0.75)
            fetch_d(t, 0)
            right_term(t, 0)
            if t < FUSED:
                right_term(t, 1)
            left_term(t, 0)
        for t in range(PACK):
            fetch_d(t, 1)
        left_term(0, 1)
        subtract(0)
        left_term(1, 1)
        second_product(0)
        for t in range(2, PACK):
            left_term(t, 1)
        for t in range(FUSED, PACK):
            right_term_shared(t, 1)
        for t in range(PACK):
            tanh_out(t, 0)
            h_out(t, 0)
        subtract(1)
        second_product(1)

        out_rows = out_0.rearrange("(p t) c -> p t c", t=PACK)
        out_words = words_view(out_1)
        out_plane = sb("out_plane", [P, H], U8)
        h_n3 = [sb(f"h_n3_{u}", [P, PACK, HALF], F32) for u in range(HALVES)]
        gated = [sb(f"gated{t}", [P, H], F32) for t in range(PACK)]
        result = [sb(f"result{u}", [P, PACK, HALF], F32) for u in range(HALVES)]

        def finish(t, u):
            nc.scalar.activation(h_n3[u][:, t, :], h_and_dn2[t][:].indirect(half_offsets(n3_sb, u)), ACT.Copy)
            nc.vector.tensor_tensor(result[u][:, t, :], gated[t][:, half_cols(u)], h_n3[u][:, t, :], ALU.mult)

        tanh_out(0, 1)
        h_out(0, 1)
        for t in range(PACK):
            if t == 0:
                for u in range(HALVES):
                    nc.vector.tensor_tensor(
                        gated[t][:, half_cols(u)],
                        tanh_and_d[t][:].indirect(half_offsets(n4_sb, u)),
                        h_and_dn2[t][:, half_cols(u)],
                        ALU.mult,
                    )
            else:
                nc.vector.tensor_tensor(
                    gated[t][:], tanh_and_d[t][:].indirect(n4_sb[:]), h_and_dn2[t][:, :H], ALU.mult
                )
            if t + 1 < PACK:
                tanh_out(t + 1, 1)
                h_out(t + 1, 1)
            if t > 0:
                finish(t - 1, 0)
        finish(PACK - 1, 0)
        nc.sync.dma_start(out_rows[:, :, half_cols(0)], result[0][:])
        for t in range(PACK):
            finish(t, 1)
        nc.sync.dma_start(out_rows[:, :, half_cols(1)], result[1][:])

        out_bf = [sb(f"out_bf{u}", [P, HALF, PACK], BF16) for u in range(HALVES)]
        nc.scalar.copy(woven(out_bf[0]), planar(result[0]))
        nc.vector.tensor_copy(woven(out_bf[1]), planar(result[1]))
        for u in reversed(range(HALVES)):
            cols = half_cols(u)
            out_codes = sb(f"out_codes{u}", [P, HALF], U32)
            nc.vector.quantize_mx(
                out_codes[:].bitcast(FP8X4), out_plane[:, cols], out_bf[u][:].rearrange("p c t -> p (c t)")
            )
            nc.sync.dma_start(out_words[:, cols], out_codes[:].bitcast(I32))
        for q in range(4):
            queue = nc.scalar if q % 2 else nc.sync
            queue.dma_start(
                out_2[0, 4 * q : 4 * q + 4, :].bitcast(I32), out_plane[32 * q : 32 * q + 4, :].bitcast(I32)
            )
